import numpy as np
import ml_dtypes


def mxq(x, axis, fmt="e4m3"):
    dtype, down = {"e4m3": (ml_dtypes.float8_e4m3fn, 7), "e5m2": (ml_dtypes.float8_e5m2, 14)}[fmt]
    v = np.moveaxis(np.asarray(x, np.float32).astype(ml_dtypes.bfloat16).astype(np.float64), axis, -1)
    blocks = v.reshape(v.shape[:-1] + (-1, 32))
    amax = np.abs(blocks).max(-1, keepdims=True)
    byte = np.maximum(np.where(amax > 0, np.frexp(amax)[1] - 1 + 127, 0) - down, 1)
    scale = np.exp2(byte - 127.0)
    codes = (blocks / scale).astype(np.float32).astype(dtype).astype(np.float64)
    return np.moveaxis((codes * scale).reshape(v.shape), -1, axis)


WIDE = False


def mx_kscale(k):
    if not WIDE:
        return np.ones(k)
    levels = np.array([30, -30])
    if k % 512:
        return np.exp2(np.random.permutation(np.resize(levels, k // 32))).repeat(32)
    a = np.empty((k // 512, 16))
    for p in range(k // 512):
        a[p, :8] = np.random.permutation(np.resize(levels, 8))
        for g in range(8):
            far = levels[np.abs(levels - a[p, g]) >= 10]
            a[p, g + 8] = far[np.random.randint(len(far))]
    return np.exp2(a.ravel()).repeat(32)


def f64(x):
    return np.asarray(x).astype(np.float64)


def striped(idx):
    return np.tile(np.asarray(idx).reshape(-1, 16).T, (8, 1)).astype(np.uint16)


def unstriped(offs):
    return offs[:16].T.reshape(-1).astype(np.int64)


E2M1 = np.array([0.0, 0.5, 1.0, 1.5, 2.0, 3.0, 4.0, 6.0, -0.0, -0.5, -1.0, -1.5, -2.0, -3.0, -4.0, -6.0])


def pack_weight(w, fmt):
    k, n = w.shape
    w = f64(np.asarray(w, np.float32).astype(ml_dtypes.bfloat16)).reshape(k // 32, 32, n)
    amax = np.abs(w).max(1)
    if fmt == "e4m3":
        byte = np.frexp(amax)[1] - 1 + 127 - 7
    else:
        mant, ex = np.frexp(amax / 6.0)
        byte = np.where(mant > 0.5, ex, ex - 1) + 127
    byte = np.clip(np.where(amax > 0, byte, 1), 1, 254)
    scaled = (w * np.exp2(127.0 - byte)[:, None, :]).reshape(k, n).astype(np.float32)
    by_word = np.ascontiguousarray(scaled.reshape(k // 512, 128, 4, n).transpose(0, 1, 3, 2))
    if fmt == "e4m3":
        words = by_word.astype(ml_dtypes.float8_e4m3fn).view(np.uint8)
    else:
        c = by_word.astype(ml_dtypes.float4_e2m1fn).view(np.uint8) & 0xF
        words = (c[..., 0::2] | (c[..., 1::2] << 4)).reshape(k // 512, 128, 2 * n)
    return np.ascontiguousarray(words), np.ascontiguousarray(byte.astype(np.uint8).reshape(k // 512, 16, n))


def unpack_weight(words, scales, fmt):
    g, _, n = scales.shape
    words = np.ascontiguousarray(words).reshape(g, 128, n, -1)
    if fmt == "e4m3":
        vals = words.view(ml_dtypes.float8_e4m3fn).astype(np.float64)
    else:
        nib = np.empty((g, 128, n, 4), np.uint8)
        nib[..., 0::2] = words & 0xF
        nib[..., 1::2] = words >> 4
        vals = E2M1[nib]
    vals = vals * np.repeat(np.exp2(scales.astype(np.float64) - 127.0), 8, axis=1)[..., None]
    return vals.transpose(0, 1, 3, 2).reshape(g * 512, n)


K, T, J, R, O, N = 512, 512, 256, 512, 128, 256


def setup_inputs():
    n = np.random.standard_normal
    idx = np.random.permutation(T)[:J]
    idx2 = np.random.permutation(J)[:O]
    idx3 = np.random.permutation(J)[:O]
    fk = mx_kscale(K)
    fr = mx_kscale(R)
    wp = pack_weight(n((K, R)) * 1 / np.sqrt(K) * fk[:, None] * fr, "e2m1")
    wbp = pack_weight(n((R, N)) * 1 / np.sqrt(R) / fr[:, None], "e4m3")
    return {
        "xf": (n((K, T))).astype(np.float32),
        "fk": (np.random.uniform(0.5, 2.0, (K, 1)) / fk[:, None]).astype(np.float32),
        "w_words": wp[0],
        "w_scales": wp[1],
        "wb_words": wbp[0],
        "wb_scales": wbp[1],
        "rs": (1.0 * n((O, N))).astype(np.float32),
        "offs": striped(idx),
        "offs2": striped(idx2),
        "offs3": striped(idx3),
    }


def reference(xf, fk, w_words, w_scales, wb_words, wb_scales, rs, offs, offs2, offs3):
    idx = unstriped(offs)
    idx2 = unstriped(offs2)
    idx3 = unstriped(offs3)
    wu = unpack_weight(w_words, w_scales, "e2m1")
    wbu = unpack_weight(wb_words, wb_scales, "e4m3")
    xg = f64(xf)[:, idx]
    x1 = np.pad(xg, ((0, 0), (1, 0)))[:, :J]
    u = (xg - 0.6 * x1) * f64(fk)
    uq = mxq(u, 0, "e4m3")
    a = wu.T @ uq
    hid = np.maximum(a[:, idx2], a[:, idx3])
    hidq = mxq(hid, 0, "e5m2")
    p = hidq.T @ wbu
    pk2 = np.max(np.abs(p), axis=1, keepdims=True)
    y = p / (pk2 + 0.2) + 0.3 * f64(rs)
    return y

@@ -1,0 +1,191 @@
+from contextlib import ExitStack
+
+import concourse.mybir as mybir
+
+K, T, J, R, O, N = 512, 512, 256, 512, 128, 256
+FLOPS = 2 * K * R * J + 2 * R * O * N
+
+F32 = mybir.dt.float32
+BF16 = mybir.dt.bfloat16
+I32 = mybir.dt.int32
+U32 = mybir.dt.uint32
+U16 = mybir.dt.uint16
+U8 = mybir.dt.uint8
+E4M3 = mybir.dt.float8_e4m3fn_x4
+E5M2 = mybir.dt.float8_e5m2_x4
+E2M1 = mybir.dt.float4_e2m1fn_x4
+ALU = mybir.AluOpType
+ACT = mybir.ActivationFunctionType
+
+P = 128
+PACK = 4
+PAD = 8
+HALF = J // 2
+
+
+def tile_list_looks_steps_larger_rowpeaks_kernel(
+    tc, xf, fk, w_words, w_scales, wb_words, wb_scales, rs, offs, offs2, offs3, out
+):
+    nc = tc.nc
+    with ExitStack() as ctx:
+        sb = ctx.enter_context(tc.tile_pool(name="sb", bufs=1))
+        ps = ctx.enter_context(tc.psum_pool(name="ps", bufs=1))
+
+        x_rows = xf.rearrange("(p t) c -> p t c", t=PACK)
+        x_pair = [sb.tile([P, 2, T], F32, name=f"x_pair{i}") for i in range(2)]
+        for i in range(2):
+            nc.scalar.dma_start(out=x_pair[i][:], in_=x_rows[:, 2 * i : 2 * i + 2, :])
+
+        list1 = sb.tile([P, J // 16], U16)
+        nc.sync.dma_start(list1[:], offs)
+        ws_raw = sb.tile([P, R], U8, align_bytes=64)
+        ws_rows = w_scales[0].bitcast(I32)
+        for q in range(4):
+            nc.sync.dma_start(
+                out=ws_raw[32 * q : 32 * q + 32, :].bitcast(I32),
+                in_=ws_rows[4 * q : 4 * q + 4, :].unsqueeze(0).to_broadcast([8, 4, R // 4]),
+            )
+        w_raw = sb.tile([P, 2 * R], U8, align_bytes=64)
+        nc.sync.dma_start(out=w_raw[:].bitcast(I32), in_=w_words[0].bitcast(I32))
+        factor = sb.tile([P, PACK], F32)
+        nc.gpsimd.dma_start(out=factor[:], in_=fk.rearrange("(p t) o -> p (t o)", t=PACK))
+
+        list2 = sb.tile([P, O // 16], U16)
+        nc.sync.dma_start(list2[:], offs2)
+        list3 = sb.tile([P, O // 16], U16)
+        nc.sync.dma_start(list3[:], offs3)
+        wb_codes = sb.tile([P, N], U32, align_bytes=64)
+        nc.sync.dma_start(
+            out=wb_codes[:].bitcast(I32), in_=wb_words[0].rearrange("p n t -> p (n t)").bitcast(I32)
+        )
+        wb_plane = sb.tile([P, N], U8, align_bytes=64)
+        nc.vector.memset(wb_plane[:].bitcast(U32), 0)
+        wbs_rows = wb_scales[0].bitcast(I32)
+        for q in range(4):
+            nc.sync.dma_start(
+                out=wb_plane[32 * q : 32 * q + 4, :].bitcast(I32), in_=wbs_rows[4 * q : 4 * q + 4, :]
+            )
+        resid = sb.tile([P, N], F32)
+        nc.sync.dma_start(out=resid[:], in_=rs)
+
+        w_codes = sb.tile([P, 2 * R], U8, align_bytes=64)
+        nc.vector.tensor_copy(
+            out=w_codes[:].bitcast(U16).rearrange("p (t m) -> p m t", t=PACK),
+            in_=w_raw[:].bitcast(U16).rearrange("p (m t) -> p m t", t=PACK),
+        )
+        w_plane = sb.tile([P, R], U8, align_bytes=64)
+        nc.vector.tensor_copy(
+            out=w_plane[:].rearrange("p (t m) -> p m t", t=PACK),
+            in_=ws_raw[:].rearrange("p (m t) -> p m t", t=PACK),
+        )
+
+        picked = sb.tile([P, PACK, J], F32)
+        scaled = sb.tile([P, PACK, PAD + J], F32)
+        nc.vector.memset(scaled[:, :, 0:PAD], 0.0)
+        for t in range(PACK):
+            window = x_pair[t // 2][:, t % 2, :].indirect(list1[:])
+            if t % 2 == 0:
+                nc.vector.tensor_copy(out=picked[:, t, :], in_=window)
+                nc.vector.tensor_scalar(
+                    out=scaled[:, t, PAD:], in0=picked[:, t, :], scalar1=factor[:, t : t + 1],
+                    scalar2=None, op0=ALU.mult,
+                )
+            else:
+                nc.scalar.activation(out=picked[:, t, :], in_=window, func=ACT.Copy)
+                nc.scalar.activation(
+                    out=scaled[:, t, PAD:], in_=picked[:, t, :], func=ACT.Copy, scale=factor[:, t : t + 1]
+                )
+
+        u_half, u_codes, u_plane = [], [], []
+        for h in range(2):
+            u_half.append(sb.tile([P, HALF, PACK], BF16, name=f"u_half{h}", align_bytes=64))
+            u_codes.append(sb.tile([P, HALF], U32, name=f"u_codes{h}", align_bytes=64))
+            u_plane.append(sb.tile([P, HALF], U8, name=f"u_plane{h}", align_bytes=64))
+            lo = PAD + h * HALF
+            nc.vector.scalar_tensor_tensor(
+                out=u_half[h][:],
+                in0=scaled[:, :, lo - 1 : lo - 1 + HALF].rearrange("p t j -> p j t"),
+                scalar=-0.6,
+                in1=scaled[:, :, lo : lo + HALF].rearrange("p t j -> p j t"),
+                op0=ALU.mult,
+                op1=ALU.add,
+            )
+        for h in range(2):
+            nc.vector.quantize_mx(
+                out=u_codes[h][:].bitcast(E4M3),
+                scales=u_plane[h][:],
+                in_=u_half[h][:].rearrange("p j t -> p (j t)"),
+            )
+
+        a_pair = [sb.tile([P, 2, J], F32, name=f"a_pair{i}") for i in range(2)]
+        for h in range(2):
+            for i in range(2):
+                bank = ps.tile([P, 2, HALF], F32, name=f"a_bank{h}{i}")
+                for e in range(2):
+                    t = 2 * i + e
+                    nc.tensor.matmul_mx(
+                        out=bank[:, e, :],
+                        lhsT=w_codes[:, 2 * P * t : 2 * P * (t + 1)].bitcast(E2M1),
+                        lhsT_scale=w_plane[:, P * t : P * (t + 1)],
+                        rhs=u_codes[h][:].bitcast(E4M3),
+                        rhs_scale=u_plane[h][:],
+                        start=True,
+                        stop=True,
+                    )
+                dst = a_pair[i][:, :, h * HALF : (h + 1) * HALF]
+                if h == 1 and i == 1:
+                    nc.vector.tensor_copy(out=dst, in_=bank[:])
+                else:
+                    nc.scalar.activation(out=dst, in_=bank[:], func=ACT.Copy)
+
+        look2 = sb.tile([P, PACK, O], F32)
+        look3 = sb.tile([P, PACK, O], F32)
+        for t in range(PACK):
+            for look, offsets in ((look2, list2), (look3, list3)):
+                window = a_pair[t // 2][:, t % 2, :].indirect(offsets[:])
+                if t < 2:
+                    nc.scalar.activation(out=look[:, t, :], in_=window, func=ACT.Copy)
+                else:
+                    nc.vector.tensor_copy(out=look[:, t, :], in_=window)
+
+        hid = sb.tile([P, O, PACK], BF16, align_bytes=64)
+        nc.vector.tensor_tensor(
+            out=hid[:].rearrange("p (c i) t -> p c t i", i=4),
+            in0=look2[:].rearrange("p t (c i) -> p c t i", i=4),
+            in1=look3[:].rearrange("p t (c i) -> p c t i", i=4),
+            op=ALU.max,
+        )
+        hid_codes = sb.tile([P, O], U32, align_bytes=64)
+        hid_plane = sb.tile([P, O], U8, align_bytes=64)
+        nc.vector.quantize_mx(
+            out=hid_codes[:].bitcast(E5M2), scales=hid_plane[:], in_=hid[:].rearrange("p o t -> p (o t)")
+        )
+
+        resid3 = sb.tile([P, N], F32)
+        nc.scalar.activation(out=resid3[:], in_=resid[:], func=ACT.Copy, scale=0.3)
+
+        prod = ps.tile([P, N], F32)
+        nc.tensor.matmul_mx(
+            out=prod[:],
+            lhsT=hid_codes[:].bitcast(E5M2),
+            lhsT_scale=hid_plane[:],
+            rhs=wb_codes[:].bitcast(E4M3),
+            rhs_scale=wb_plane[:],
+            start=True,
+            stop=True,
+        )
+        size = sb.tile([P, N], F32)
+        nc.scalar.activation(out=size[:], in_=prod[:], func=ACT.Abs)
+        lifted = sb.tile([P, N], F32)
+        denom = sb.tile([P, 1], F32)
+        nc.vector.tensor_scalar(
+            out=lifted[:], in0=size[:], scalar1=0.2, scalar2=None, op0=ALU.add, op1=ALU.max,
+            accum_out=denom[:],
+        )
+        inverse = sb.tile([P, 1], F32)
+        nc.vector.reciprocal(out=inverse[:], in_=denom[:])
+        result = sb.tile([P, N], F32)
+        nc.vector.scalar_tensor_tensor(
+            out=result[:], in0=prod[:], scalar=inverse[:], in1=resid3[:], op0=ALU.mult, op1=ALU.add
+        )
+        nc.sync.dma_start(out=out, in_=result[:])

@@ -32,23 +32,29 @@ def tile_list_looks_steps_larger_rowpeaks_kernel(
         ps = ctx.enter_context(tc.psum_pool(name="ps", bufs=1))
 
         x_rows = xf.rearrange("(p t) c -> p t c", t=PACK)
-        x_pair = [sb.tile([P, 2, T], F32, name=f"x_pair{i}") for i in range(2)]
-        for i in range(2):
-            nc.scalar.dma_start(out=x_pair[i][:], in_=x_rows[:, 2 * i : 2 * i + 2, :])
-
+        x_plane = [sb.tile([P, T], F32, name=f"x_plane{t}") for t in range(PACK)]
         list1 = sb.tile([P, J // 16], U16)
-        nc.sync.dma_start(list1[:], offs)
+        factor = sb.tile([P, PACK], F32)
         ws_raw = sb.tile([P, R], U8, align_bytes=64)
+        w_raw = sb.tile([P, 2 * R], U8, align_bytes=64)
         ws_rows = w_scales[0].bitcast(I32)
-        for q in range(4):
-            nc.sync.dma_start(
+
+        def load_scale_rows(queue, q):
+            queue.dma_start(
                 out=ws_raw[32 * q : 32 * q + 32, :].bitcast(I32),
                 in_=ws_rows[4 * q : 4 * q + 4, :].unsqueeze(0).to_broadcast([8, 4, R // 4]),
             )
-        w_raw = sb.tile([P, 2 * R], U8, align_bytes=64)
+
+        nc.sync.dma_start(list1[:], offs)
+        load_scale_rows(nc.scalar, 0)
+        nc.sync.dma_start(out=x_plane[0][:], in_=x_rows[:, 0, :])
+        load_scale_rows(nc.scalar, 1)
+        nc.sync.dma_start(out=factor[:], in_=fk.rearrange("(p t) o -> p (t o)", t=PACK))
+        for t in range(1, PACK):
+            nc.sync.dma_start(out=x_plane[t][:], in_=x_rows[:, t, :])
         nc.sync.dma_start(out=w_raw[:].bitcast(I32), in_=w_words[0].bitcast(I32))
-        factor = sb.tile([P, PACK], F32)
-        nc.gpsimd.dma_start(out=factor[:], in_=fk.rearrange("(p t) o -> p (t o)", t=PACK))
+        load_scale_rows(nc.sync, 2)
+        load_scale_rows(nc.sync, 3)
 
         list2 = sb.tile([P, O // 16], U16)
         nc.sync.dma_start(list2[:], offs2)
@@ -68,39 +74,46 @@ def tile_list_looks_steps_larger_rowpeaks_kernel(
         resid = sb.tile([P, N], F32)
         nc.sync.dma_start(out=resid[:], in_=rs)
 
-        w_codes = sb.tile([P, 2 * R], U8, align_bytes=64)
-        nc.vector.tensor_copy(
-            out=w_codes[:].bitcast(U16).rearrange("p (t m) -> p m t", t=PACK),
-            in_=w_raw[:].bitcast(U16).rearrange("p (m t) -> p m t", t=PACK),
-        )
-        w_plane = sb.tile([P, R], U8, align_bytes=64)
-        nc.vector.tensor_copy(
-            out=w_plane[:].rearrange("p (t m) -> p m t", t=PACK),
-            in_=ws_raw[:].rearrange("p (m t) -> p m t", t=PACK),
-        )
-
-        picked = sb.tile([P, PACK, J], F32)
         scaled = sb.tile([P, PACK, PAD + J], F32)
-        nc.vector.memset(scaled[:, :, 0:PAD], 0.0)
+        zeros = sb.tile([P, PACK, PAD], F32)
+        nc.vector.memset(zeros[:], 0.0)
+        nc.scalar.activation(out=scaled[:, :, 0:PAD], in_=zeros[:], func=ACT.Copy)
+        spread = {}
+        for t in (1, 3):
+            spread[t] = sb.tile([P, J], F32, name=f"spread{t}")
+            nc.vector.tensor_copy(out=spread[t][:], in_=factor[:, t : t + 1].to_broadcast([P, J]))
+
+        w_plane = [sb.tile([P, 2 * P], U8, name=f"w_plane{i}", align_bytes=64) for i in range(2)]
+        w_codes = [sb.tile([P, 4 * P], U8, name=f"w_codes{i}", align_bytes=64) for i in range(2)]
         for t in range(PACK):
-            window = x_pair[t // 2][:, t % 2, :].indirect(list1[:])
-            if t % 2 == 0:
-                nc.vector.tensor_copy(out=picked[:, t, :], in_=window)
-                nc.vector.tensor_scalar(
-                    out=scaled[:, t, PAD:], in0=picked[:, t, :], scalar1=factor[:, t : t + 1],
-                    scalar2=None, op0=ALU.mult,
-                )
+            window = x_plane[t][:].indirect(list1[:])
+            if t % 2 == 1:
+                nc.vector.tensor_tensor(out=scaled[:, t, PAD:], in0=window, in1=spread[t][:], op=ALU.mult)
             else:
-                nc.scalar.activation(out=picked[:, t, :], in_=window, func=ACT.Copy)
+                picked = sb.tile([P, J], F32, name=f"picked{t}")
+                nc.scalar.activation(out=picked[:], in_=window, func=ACT.Copy)
                 nc.scalar.activation(
-                    out=scaled[:, t, PAD:], in_=picked[:, t, :], func=ACT.Copy, scale=factor[:, t : t + 1]
+                    out=scaled[:, t, PAD:], in_=picked[:], func=ACT.Copy, scale=factor[:, t : t + 1]
                 )
 
-        u_half, u_codes, u_plane = [], [], []
+        def deal_weights(i):
+            slots = slice(2 * i, 2 * i + 2)
+            nc.vector.tensor_copy(
+                out=w_codes[i][:].bitcast(U16).rearrange("p (t m) -> p m t", t=2),
+                in_=w_raw[:].bitcast(U16).rearrange("p (m t) -> p m t", t=PACK)[:, :, slots],
+            )
+            nc.vector.tensor_copy(
+                out=w_plane[i][:].rearrange("p (t m) -> p m t", t=2),
+                in_=ws_raw[:].rearrange("p (m t) -> p m t", t=PACK)[:, :, slots],
+            )
+
+        deal_weights(0)
+
+        u_codes = sb.tile([P, J], U32, align_bytes=64)
+        u_plane = sb.tile([P, J], U8, align_bytes=64)
+        u_half = []
         for h in range(2):
             u_half.append(sb.tile([P, HALF, PACK], BF16, name=f"u_half{h}", align_bytes=64))
-            u_codes.append(sb.tile([P, HALF], U32, name=f"u_codes{h}", align_bytes=64))
-            u_plane.append(sb.tile([P, HALF], U8, name=f"u_plane{h}", align_bytes=64))
             lo = PAD + h * HALF
             nc.vector.scalar_tensor_tensor(
                 out=u_half[h][:],
@@ -111,39 +124,39 @@ def tile_list_looks_steps_larger_rowpeaks_kernel(
                 op1=ALU.add,
             )
         for h in range(2):
+            cols = slice(h * HALF, (h + 1) * HALF)
             nc.vector.quantize_mx(
-                out=u_codes[h][:].bitcast(E4M3),
-                scales=u_plane[h][:],
+                out=u_codes[:, cols].bitcast(E4M3),
+                scales=u_plane[:, cols],
                 in_=u_half[h][:].rearrange("p j t -> p (j t)"),
             )
 
-        a_pair = [sb.tile([P, 2, J], F32, name=f"a_pair{i}") for i in range(2)]
-        for h in range(2):
-            for i in range(2):
-                bank = ps.tile([P, 2, HALF], F32, name=f"a_bank{h}{i}")
-                for e in range(2):
-                    t = 2 * i + e
-                    nc.tensor.matmul_mx(
-                        out=bank[:, e, :],
-                        lhsT=w_codes[:, 2 * P * t : 2 * P * (t + 1)].bitcast(E2M1),
-                        lhsT_scale=w_plane[:, P * t : P * (t + 1)],
-                        rhs=u_codes[h][:].bitcast(E4M3),
-                        rhs_scale=u_plane[h][:],
-                        start=True,
-                        stop=True,
-                    )
-                dst = a_pair[i][:, :, h * HALF : (h + 1) * HALF]
-                if h == 1 and i == 1:
-                    nc.vector.tensor_copy(out=dst, in_=bank[:])
-                else:
-                    nc.scalar.activation(out=dst, in_=bank[:], func=ACT.Copy)
+        deal_weights(1)
+
+        a_rows = []
+        for t in range(PACK):
+            bank = ps.tile([P, J], F32, name=f"a_bank{t}")
+            nc.tensor.matmul_mx(
+                out=bank[:],
+                lhsT=w_codes[t // 2][:, 2 * P * (t % 2) : 2 * P * (t % 2 + 1)].bitcast(E2M1),
+                lhsT_scale=w_plane[t // 2][:, P * (t % 2) : P * (t % 2 + 1)],
+                rhs=u_codes[:].bitcast(E4M3),
+                rhs_scale=u_plane[:],
+                start=True,
+                stop=True,
+            )
+            a_rows.append(sb.tile([P, J], F32, name=f"a_rows{t}"))
+            if t % 2 == 1:
+                nc.vector.tensor_copy(out=a_rows[t][:], in_=bank[:])
+            else:
+                nc.scalar.activation(out=a_rows[t][:], in_=bank[:], func=ACT.Copy)
 
         look2 = sb.tile([P, PACK, O], F32)
         look3 = sb.tile([P, PACK, O], F32)
         for t in range(PACK):
             for look, offsets in ((look2, list2), (look3, list3)):
-                window = a_pair[t // 2][:, t % 2, :].indirect(offsets[:])
-                if t < 2:
+                window = a_rows[t][:].indirect(offsets[:])
+                if t % 2 == 0:
                     nc.scalar.activation(out=look[:, t, :], in_=window, func=ACT.Copy)
                 else:
                     nc.vector.tensor_copy(out=look[:, t, :], in_=window)
@@ -184,8 +197,11 @@ def tile_list_looks_steps_larger_rowpeaks_kernel(
         )
         inverse = sb.tile([P, 1], F32)
         nc.vector.reciprocal(out=inverse[:], in_=denom[:])
-        result = sb.tile([P, N], F32)
-        nc.vector.scalar_tensor_tensor(
-            out=result[:], in0=prod[:], scalar=inverse[:], in1=resid3[:], op0=ALU.mult, op1=ALU.add
-        )
-        nc.sync.dma_start(out=out, in_=result[:])
+        for h, queue in enumerate((nc.scalar, nc.sync)):
+            cols = slice(h * (N // 2), (h + 1) * (N // 2))
+            result = sb.tile([P, N // 2], F32, name=f"result{h}")
+            nc.vector.scalar_tensor_tensor(
+                out=result[:], in0=prod[:, cols], scalar=inverse[:], in1=resid3[:, cols],
+                op0=ALU.mult, op1=ALU.add,
+            )
+            queue.dma_start(out=out[:, cols], in_=result[:])

@@ -46,16 +46,22 @@ def tile_list_looks_steps_larger_rowpeaks_kernel(
             )
 
         nc.sync.dma_start(list1[:], offs)
-        load_scale_rows(nc.scalar, 0)
+        for q in range(3):
+            load_scale_rows(nc.scalar, q)
         nc.sync.dma_start(out=x_plane[0][:], in_=x_rows[:, 0, :])
-        load_scale_rows(nc.scalar, 1)
         nc.sync.dma_start(out=factor[:], in_=fk.rearrange("(p t) o -> p (t o)", t=PACK))
         for t in range(1, PACK):
             nc.sync.dma_start(out=x_plane[t][:], in_=x_rows[:, t, :])
+        scaled = [sb.tile([P, 2, PAD + J], F32, name=f"scaled{i}") for i in range(2)]
+        zeros = sb.tile([P, 2, PAD], F32)
+        nc.vector.memset(zeros[:], 0.0)
+        for i in range(2):
+            nc.scalar.activation(out=scaled[i][:, :, 0:PAD], in_=zeros[:], func=ACT.Copy)
+        load_scale_rows(nc.scalar, 3)
         nc.sync.dma_start(out=w_raw[:].bitcast(I32), in_=w_words[0].bitcast(I32))
-        load_scale_rows(nc.sync, 2)
-        load_scale_rows(nc.sync, 3)
 
+        resid = sb.tile([P, N], F32)
+        nc.sync.dma_start(out=resid[:], in_=rs)
         list2 = sb.tile([P, O // 16], U16)
         nc.sync.dma_start(list2[:], offs2)
         list3 = sb.tile([P, O // 16], U16)
@@ -71,57 +77,73 @@ def tile_list_looks_steps_larger_rowpeaks_kernel(
             nc.sync.dma_start(
                 out=wb_plane[32 * q : 32 * q + 4, :].bitcast(I32), in_=wbs_rows[4 * q : 4 * q + 4, :]
             )
-        resid = sb.tile([P, N], F32)
-        nc.sync.dma_start(out=resid[:], in_=rs)
 
-        scaled = sb.tile([P, PACK, PAD + J], F32)
-        zeros = sb.tile([P, PACK, PAD], F32)
-        nc.vector.memset(zeros[:], 0.0)
-        nc.scalar.activation(out=scaled[:, :, 0:PAD], in_=zeros[:], func=ACT.Copy)
-        spread = {}
-        for t in (1, 3):
-            spread[t] = sb.tile([P, J], F32, name=f"spread{t}")
-            nc.vector.tensor_copy(out=spread[t][:], in_=factor[:, t : t + 1].to_broadcast([P, J]))
+        spread1 = sb.tile([P, J], F32)
+        nc.vector.tensor_copy(out=spread1[:], in_=factor[:, 1:2].to_broadcast([P, J]))
+        spread3 = sb.tile([P, HALF], F32)
+        nc.vector.tensor_copy(out=spread3[:], in_=factor[:, 3:4].to_broadcast([P, HALF]))
 
-        w_plane = [sb.tile([P, 2 * P], U8, name=f"w_plane{i}", align_bytes=64) for i in range(2)]
-        w_codes = [sb.tile([P, 4 * P], U8, name=f"w_codes{i}", align_bytes=64) for i in range(2)]
-        for t in range(PACK):
-            window = x_plane[t][:].indirect(list1[:])
-            if t % 2 == 1:
-                nc.vector.tensor_tensor(out=scaled[:, t, PAD:], in0=window, in1=spread[t][:], op=ALU.mult)
-            else:
-                picked = sb.tile([P, J], F32, name=f"picked{t}")
-                nc.scalar.activation(out=picked[:], in_=window, func=ACT.Copy)
-                nc.scalar.activation(
-                    out=scaled[:, t, PAD:], in_=picked[:], func=ACT.Copy, scale=factor[:, t : t + 1]
+        w_plane = sb.tile([P, R], U8, align_bytes=64)
+        pairs = [sb.tile([P, 2, HALF, 2], BF16, name=f"pairs{h}") for h in range(2)]
+
+        def take_steps(i):
+            for h in range(2):
+                lo = PAD + h * HALF
+                nc.vector.scalar_tensor_tensor(
+                    out=pairs[h][:, i, :, :],
+                    in0=scaled[i][:, :, lo - 1 : lo - 1 + HALF].rearrange("p e j -> p j e"),
+                    scalar=-0.6,
+                    in1=scaled[i][:, :, lo : lo + HALF].rearrange("p e j -> p j e"),
+                    op0=ALU.mult,
+                    op1=ALU.add,
                 )
 
-        def deal_weights(i):
-            slots = slice(2 * i, 2 * i + 2)
+        picked0 = sb.tile([P, J], F32)
+        nc.scalar.activation(out=picked0[:], in_=x_plane[0][:].indirect(list1[:]), func=ACT.Copy)
+        nc.scalar.activation(out=scaled[0][:, 0, PAD:], in_=picked0[:], func=ACT.Copy, scale=factor[:, 0:1])
+        nc.vector.tensor_tensor(
+            out=scaled[0][:, 1, PAD:], in0=x_plane[1][:].indirect(list1[:]), in1=spread1[:], op=ALU.mult
+        )
+        take_steps(0)
+        picked2 = sb.tile([P, J], F32)
+        nc.scalar.activation(out=picked2[:], in_=x_plane[2][:].indirect(list1[:]), func=ACT.Copy)
+        picked3 = sb.tile([P, HALF], F32)
+        nc.scalar.activation(out=picked3[:], in_=x_plane[3][:].indirect(list1[:, HALF // 16 :]), func=ACT.Copy)
+        nc.scalar.activation(out=scaled[1][:, 0, PAD:], in_=picked2[:], func=ACT.Copy, scale=factor[:, 2:3])
+        nc.scalar.activation(
+            out=scaled[1][:, 1, PAD + HALF :], in_=picked3[:], func=ACT.Copy, scale=factor[:, 3:4]
+        )
+        nc.vector.tensor_tensor(
+            out=scaled[1][:, 1, PAD : PAD + HALF],
+            in0=x_plane[3][:].indirect(list1[:, 0 : HALF // 16]),
+            in1=spread3[:],
+            op=ALU.mult,
+        )
+        nc.vector.tensor_copy(
+            out=w_plane[:].rearrange("p (t m) -> p m t", t=PACK),
+            in_=ws_raw[:].rearrange("p (m t) -> p m t", t=PACK),
+        )
+
+        w_codes = []
+
+        def deal_words(i, tag):
+            w_codes.append(sb.tile([P, 4 * P], U8, name=f"w_codes{i}", tag=tag, align_bytes=64))
             nc.vector.tensor_copy(
                 out=w_codes[i][:].bitcast(U16).rearrange("p (t m) -> p m t", t=2),
-                in_=w_raw[:].bitcast(U16).rearrange("p (m t) -> p m t", t=PACK)[:, :, slots],
-            )
-            nc.vector.tensor_copy(
-                out=w_plane[i][:].rearrange("p (t m) -> p m t", t=2),
-                in_=ws_raw[:].rearrange("p (m t) -> p m t", t=PACK)[:, :, slots],
+                in_=w_raw[:].bitcast(U16).rearrange("p (m t) -> p m t", t=PACK)[:, :, 2 * i : 2 * i + 2],
             )
 
-        deal_weights(0)
+        deal_words(0, "w_codes0")
+        take_steps(1)
 
         u_codes = sb.tile([P, J], U32, align_bytes=64)
         u_plane = sb.tile([P, J], U8, align_bytes=64)
         u_half = []
         for h in range(2):
-            u_half.append(sb.tile([P, HALF, PACK], BF16, name=f"u_half{h}", align_bytes=64))
-            lo = PAD + h * HALF
-            nc.vector.scalar_tensor_tensor(
-                out=u_half[h][:],
-                in0=scaled[:, :, lo - 1 : lo - 1 + HALF].rearrange("p t j -> p j t"),
-                scalar=-0.6,
-                in1=scaled[:, :, lo : lo + HALF].rearrange("p t j -> p j t"),
-                op0=ALU.mult,
-                op1=ALU.add,
+            u_half.append(sb.tile([P, HALF, PACK], BF16, name=f"u_half{h}", tag=f"u_half{h}", align_bytes=64))
+            nc.vector.tensor_copy(
+                out=u_half[h][:].rearrange("p j t -> p (j t)").bitcast(I32).rearrange("p (j i) -> p j i", i=2),
+                in_=pairs[h][:].rearrange("p i j e -> p i (j e)").bitcast(I32).rearrange("p i j -> p j i"),
             )
         for h in range(2):
             cols = slice(h * HALF, (h + 1) * HALF)
@@ -131,7 +153,7 @@ def tile_list_looks_steps_larger_rowpeaks_kernel(
                 in_=u_half[h][:].rearrange("p j t -> p (j t)"),
             )
 
-        deal_weights(1)
+        deal_words(1, "u_half1")
 
         a_rows = []
         for t in range(PACK):
@@ -139,56 +161,63 @@ def tile_list_looks_steps_larger_rowpeaks_kernel(
             nc.tensor.matmul_mx(
                 out=bank[:],
                 lhsT=w_codes[t // 2][:, 2 * P * (t % 2) : 2 * P * (t % 2 + 1)].bitcast(E2M1),
-                lhsT_scale=w_plane[t // 2][:, P * (t % 2) : P * (t % 2 + 1)],
+                lhsT_scale=w_plane[:, P * t : P * (t + 1)],
                 rhs=u_codes[:].bitcast(E4M3),
                 rhs_scale=u_plane[:],
                 start=True,
                 stop=True,
             )
             a_rows.append(sb.tile([P, J], F32, name=f"a_rows{t}"))
-            if t % 2 == 1:
-                nc.vector.tensor_copy(out=a_rows[t][:], in_=bank[:])
-            else:
-                nc.scalar.activation(out=a_rows[t][:], in_=bank[:], func=ACT.Copy)
+            nc.scalar.activation(out=a_rows[t][:], in_=bank[:], func=ACT.Copy)
 
         look2 = sb.tile([P, PACK, O], F32)
         look3 = sb.tile([P, PACK, O], F32)
         for t in range(PACK):
-            for look, offsets in ((look2, list2), (look3, list3)):
+            for e, (look, offsets) in enumerate(((look2, list2), (look3, list3))):
                 window = a_rows[t][:].indirect(offsets[:])
-                if t % 2 == 0:
+                if 2 * t + e >= 5:
                     nc.scalar.activation(out=look[:, t, :], in_=window, func=ACT.Copy)
                 else:
                     nc.vector.tensor_copy(out=look[:, t, :], in_=window)
 
-        hid = sb.tile([P, O, PACK], BF16, align_bytes=64)
-        nc.vector.tensor_tensor(
-            out=hid[:].rearrange("p (c i) t -> p c t i", i=4),
-            in0=look2[:].rearrange("p t (c i) -> p c t i", i=4),
-            in1=look3[:].rearrange("p t (c i) -> p c t i", i=4),
-            op=ALU.max,
-        )
         hid_codes = sb.tile([P, O], U32, align_bytes=64)
         hid_plane = sb.tile([P, O], U8, align_bytes=64)
-        nc.vector.quantize_mx(
-            out=hid_codes[:].bitcast(E5M2), scales=hid_plane[:], in_=hid[:].rearrange("p o t -> p (o t)")
-        )
+        hid_half = []
+        for h in range(2):
+            cols = slice(h * (O // 2), (h + 1) * (O // 2))
+            hid_half.append(sb.tile([P, O // 2, PACK], BF16, name=f"hid_half{h}", align_bytes=64))
+            nc.vector.tensor_tensor(
+                out=hid_half[h][:].rearrange("p (c i) t -> p c t i", i=4),
+                in0=look2[:, :, cols].rearrange("p t (c i) -> p c t i", i=4),
+                in1=look3[:, :, cols].rearrange("p t (c i) -> p c t i", i=4),
+                op=ALU.max,
+            )
+        for h in range(2):
+            cols = slice(h * (O // 2), (h + 1) * (O // 2))
+            nc.vector.quantize_mx(
+                out=hid_codes[:, cols].bitcast(E5M2),
+                scales=hid_plane[:, cols],
+                in_=hid_half[h][:].rearrange("p o t -> p (o t)"),
+            )
 
         resid3 = sb.tile([P, N], F32)
         nc.scalar.activation(out=resid3[:], in_=resid[:], func=ACT.Copy, scale=0.3)
 
-        prod = ps.tile([P, N], F32)
-        nc.tensor.matmul_mx(
-            out=prod[:],
-            lhsT=hid_codes[:].bitcast(E5M2),
-            lhsT_scale=hid_plane[:],
-            rhs=wb_codes[:].bitcast(E4M3),
-            rhs_scale=wb_plane[:],
-            start=True,
-            stop=True,
-        )
         size = sb.tile([P, N], F32)
-        nc.scalar.activation(out=size[:], in_=prod[:], func=ACT.Abs)
+        prod = []
+        for h in range(2):
+            cols = slice(h * (N // 2), (h + 1) * (N // 2))
+            prod.append(ps.tile([P, N // 2], F32, name=f"prod{h}"))
+            nc.tensor.matmul_mx(
+                out=prod[h][:],
+                lhsT=hid_codes[:].bitcast(E5M2),
+                lhsT_scale=hid_plane[:],
+                rhs=wb_codes[:, cols].bitcast(E4M3),
+                rhs_scale=wb_plane[:, cols],
+                start=True,
+                stop=True,
+            )
+            nc.scalar.activation(out=size[:, cols], in_=prod[h][:], func=ACT.Abs)
         lifted = sb.tile([P, N], F32)
         denom = sb.tile([P, 1], F32)
         nc.vector.tensor_scalar(
@@ -201,7 +230,7 @@ def tile_list_looks_steps_larger_rowpeaks_kernel(
             cols = slice(h * (N // 2), (h + 1) * (N // 2))
             result = sb.tile([P, N // 2], F32, name=f"result{h}")
             nc.vector.scalar_tensor_tensor(
-                out=result[:], in0=prod[:, cols], scalar=inverse[:], in1=resid3[:, cols],
+                out=result[:], in0=prod[h][:], scalar=inverse[:], in1=resid3[:, cols],
                 op0=ALU.mult, op1=ALU.add,
             )
             queue.dma_start(out=out[:, cols], in_=result[:])

@@ -60,7 +60,7 @@ def tile_list_looks_steps_larger_rowpeaks_kernel(
         load_scale_rows(nc.scalar, 3)
         nc.sync.dma_start(out=w_raw[:].bitcast(I32), in_=w_words[0].bitcast(I32))
 
-        resid = sb.tile([P, N], F32)
+        resid = sb.tile([P, N], F32, tag="a_rows0")
         nc.sync.dma_start(out=resid[:], in_=rs)
         list2 = sb.tile([P, O // 16], U16)
         nc.sync.dma_start(list2[:], offs2)
@@ -120,8 +120,8 @@ def tile_list_looks_steps_larger_rowpeaks_kernel(
             op=ALU.mult,
         )
         nc.vector.tensor_copy(
-            out=w_plane[:].rearrange("p (t m) -> p m t", t=PACK),
-            in_=ws_raw[:].rearrange("p (m t) -> p m t", t=PACK),
+            out=w_plane[:].rearrange("p (t m) -> p t m", t=PACK),
+            in_=ws_raw[:].rearrange("p (m t) -> p t m", t=PACK),
         )
 
         w_codes = []
@@ -129,8 +129,8 @@ def tile_list_looks_steps_larger_rowpeaks_kernel(
         def deal_words(i, tag):
             w_codes.append(sb.tile([P, 4 * P], U8, name=f"w_codes{i}", tag=tag, align_bytes=64))
             nc.vector.tensor_copy(
-                out=w_codes[i][:].bitcast(U16).rearrange("p (t m) -> p m t", t=2),
-                in_=w_raw[:].bitcast(U16).rearrange("p (m t) -> p m t", t=PACK)[:, :, 2 * i : 2 * i + 2],
+                out=w_codes[i][:].bitcast(U16).rearrange("p (t m) -> p t m", t=2),
+                in_=w_raw[:].bitcast(U16).rearrange("p (m t) -> p t m", t=PACK)[:, 2 * i : 2 * i + 2, :],
             )
 
         deal_words(0, "w_codes0")
@@ -153,21 +153,25 @@ def tile_list_looks_steps_larger_rowpeaks_kernel(
                 in_=u_half[h][:].rearrange("p j t -> p (j t)"),
             )
 
-        deal_words(1, "u_half1")
+        deal_words(1, "u_half0")
+
+        resid3 = sb.tile([P, N], F32)
+        nc.scalar.activation(out=resid3[:], in_=resid[:], func=ACT.Copy, scale=0.3)
 
         a_rows = []
         for t in range(PACK):
             bank = ps.tile([P, J], F32, name=f"a_bank{t}")
-            nc.tensor.matmul_mx(
-                out=bank[:],
-                lhsT=w_codes[t // 2][:, 2 * P * (t % 2) : 2 * P * (t % 2 + 1)].bitcast(E2M1),
-                lhsT_scale=w_plane[:, P * t : P * (t + 1)],
-                rhs=u_codes[:].bitcast(E4M3),
-                rhs_scale=u_plane[:],
-                start=True,
-                stop=True,
-            )
-            a_rows.append(sb.tile([P, J], F32, name=f"a_rows{t}"))
+            for cols in [slice(0, HALF), slice(HALF, J)] if t == 0 else [slice(0, J)]:
+                nc.tensor.matmul_mx(
+                    out=bank[:, cols],
+                    lhsT=w_codes[t // 2][:, 2 * P * (t % 2) : 2 * P * (t % 2 + 1)].bitcast(E2M1),
+                    lhsT_scale=w_plane[:, P * t : P * (t + 1)],
+                    rhs=u_codes[:, cols].bitcast(E4M3),
+                    rhs_scale=u_plane[:, cols],
+                    start=True,
+                    stop=True,
+                )
+            a_rows.append(sb.tile([P, J], F32, name=f"a_rows{t}", tag=f"a_rows{t}"))
             nc.scalar.activation(out=a_rows[t][:], in_=bank[:], func=ACT.Copy)
 
         look2 = sb.tile([P, PACK, O], F32)
@@ -199,9 +203,6 @@ def tile_list_looks_steps_larger_rowpeaks_kernel(
                 scales=hid_plane[:, cols],
                 in_=hid_half[h][:].rearrange("p o t -> p (o t)"),
             )
-
-        resid3 = sb.tile([P, N], F32)
-        nc.scalar.activation(out=resid3[:], in_=resid[:], func=ACT.Copy, scale=0.3)
 
         size = sb.tile([P, N], F32)
         prod = []

from contextlib import ExitStack

import concourse.mybir as mybir

K, T, J, R, O, N = 512, 512, 256, 512, 128, 256
FLOPS = 2 * K * R * J + 2 * R * O * N

F32 = mybir.dt.float32
BF16 = mybir.dt.bfloat16
I32 = mybir.dt.int32
U32 = mybir.dt.uint32
U16 = mybir.dt.uint16
U8 = mybir.dt.uint8
E4M3 = mybir.dt.float8_e4m3fn_x4
E5M2 = mybir.dt.float8_e5m2_x4
E2M1 = mybir.dt.float4_e2m1fn_x4
ALU = mybir.AluOpType
ACT = mybir.ActivationFunctionType

P = 128
PACK = 4
PAD = 8
HALF = J // 2


def tile_list_looks_steps_larger_rowpeaks_kernel(
    tc, xf, fk, w_words, w_scales, wb_words, wb_scales, rs, offs, offs2, offs3, out
):
    nc = tc.nc
    with ExitStack() as ctx:
        sb = ctx.enter_context(tc.tile_pool(name="sb", bufs=1))
        ps = ctx.enter_context(tc.psum_pool(name="ps", bufs=1))

        x_rows = xf.rearrange("(p t) c -> p t c", t=PACK)
        x_plane = [sb.tile([P, T], F32, name=f"x_plane{t}") for t in range(PACK)]
        list1 = sb.tile([P, J // 16], U16)
        factor = sb.tile([P, PACK], F32)
        ws_raw = sb.tile([P, R], U8, align_bytes=64)
        w_raw = sb.tile([P, 2 * R], U8, align_bytes=64)
        ws_rows = w_scales[0].bitcast(I32)

        def load_scale_rows(queue, q):
            queue.dma_start(
                out=ws_raw[32 * q : 32 * q + 32, :].bitcast(I32),
                in_=ws_rows[4 * q : 4 * q + 4, :].unsqueeze(0).to_broadcast([8, 4, R // 4]),
            )

        nc.sync.dma_start(list1[:], offs)
        for q in range(3):
            load_scale_rows(nc.scalar, q)
        nc.sync.dma_start(out=x_plane[0][:], in_=x_rows[:, 0, :])
        nc.sync.dma_start(out=factor[:], in_=fk.rearrange("(p t) o -> p (t o)", t=PACK))
        for t in range(1, PACK):
            nc.sync.dma_start(out=x_plane[t][:], in_=x_rows[:, t, :])
        scaled = [sb.tile([P, 2, PAD + J], F32, name=f"scaled{i}") for i in range(2)]
        zeros = sb.tile([P, 2, PAD], F32)
        nc.vector.memset(zeros[:], 0.0)
        for i in range(2):
            nc.scalar.activation(out=scaled[i][:, :, 0:PAD], in_=zeros[:], func=ACT.Copy)
        load_scale_rows(nc.scalar, 3)
        nc.sync.dma_start(out=w_raw[:].bitcast(I32), in_=w_words[0].bitcast(I32))

        resid = sb.tile([P, N], F32, tag="a_rows0")
        nc.sync.dma_start(out=resid[:], in_=rs)
        list2 = sb.tile([P, O // 16], U16)
        nc.sync.dma_start(list2[:], offs2)
        list3 = sb.tile([P, O // 16], U16)
        nc.sync.dma_start(list3[:], offs3)
        wb_codes = sb.tile([P, N], U32, align_bytes=64)
        nc.sync.dma_start(
            out=wb_codes[:].bitcast(I32), in_=wb_words[0].rearrange("p n t -> p (n t)").bitcast(I32)
        )
        wb_plane = sb.tile([P, N], U8, align_bytes=64)
        nc.vector.memset(wb_plane[:].bitcast(U32), 0)
        wbs_rows = wb_scales[0].bitcast(I32)
        for q in range(4):
            nc.sync.dma_start(
                out=wb_plane[32 * q : 32 * q + 4, :].bitcast(I32), in_=wbs_rows[4 * q : 4 * q + 4, :]
            )

        spread1 = sb.tile([P, J], F32)
        nc.vector.tensor_copy(out=spread1[:], in_=factor[:, 1:2].to_broadcast([P, J]))
        spread3 = sb.tile([P, HALF], F32)
        nc.vector.tensor_copy(out=spread3[:], in_=factor[:, 3:4].to_broadcast([P, HALF]))

        w_plane = sb.tile([P, R], U8, align_bytes=64)
        pairs = [sb.tile([P, 2, HALF, 2], BF16, name=f"pairs{h}") for h in range(2)]

        def take_steps(i):
            for h in range(2):
                lo = PAD + h * HALF
                nc.vector.scalar_tensor_tensor(
                    out=pairs[h][:, i, :, :],
                    in0=scaled[i][:, :, lo - 1 : lo - 1 + HALF].rearrange("p e j -> p j e"),
                    scalar=-0.6,
                    in1=scaled[i][:, :, lo : lo + HALF].rearrange("p e j -> p j e"),
                    op0=ALU.mult,
                    op1=ALU.add,
                )

        picked0 = sb.tile([P, J], F32)
        nc.scalar.activation(out=picked0[:], in_=x_plane[0][:].indirect(list1[:]), func=ACT.Copy)
        nc.scalar.activation(out=scaled[0][:, 0, PAD:], in_=picked0[:], func=ACT.Copy, scale=factor[:, 0:1])
        nc.vector.tensor_tensor(
            out=scaled[0][:, 1, PAD:], in0=x_plane[1][:].indirect(list1[:]), in1=spread1[:], op=ALU.mult
        )
        take_steps(0)
        picked2 = sb.tile([P, J], F32)
        nc.scalar.activation(out=picked2[:], in_=x_plane[2][:].indirect(list1[:]), func=ACT.Copy)
        picked3 = sb.tile([P, HALF], F32)
        nc.scalar.activation(out=picked3[:], in_=x_plane[3][:].indirect(list1[:, HALF // 16 :]), func=ACT.Copy)
        nc.scalar.activation(out=scaled[1][:, 0, PAD:], in_=picked2[:], func=ACT.Copy, scale=factor[:, 2:3])
        nc.scalar.activation(
            out=scaled[1][:, 1, PAD + HALF :], in_=picked3[:], func=ACT.Copy, scale=factor[:, 3:4]
        )
        nc.vector.tensor_tensor(
            out=scaled[1][:, 1, PAD : PAD + HALF],
            in0=x_plane[3][:].indirect(list1[:, 0 : HALF // 16]),
            in1=spread3[:],
            op=ALU.mult,
        )
        nc.vector.tensor_copy(
            out=w_plane[:].rearrange("p (t m) -> p t m", t=PACK),
            in_=ws_raw[:].rearrange("p (m t) -> p t m", t=PACK),
        )

        w_codes = []

        def deal_words(i, tag):
            w_codes.append(sb.tile([P, 4 * P], U8, name=f"w_codes{i}", tag=tag, align_bytes=64))
            nc.vector.tensor_copy(
                out=w_codes[i][:].bitcast(U16).rearrange("p (t m) -> p t m", t=2),
                in_=w_raw[:].bitcast(U16).rearrange("p (m t) -> p t m", t=PACK)[:, 2 * i : 2 * i + 2, :],
            )

        deal_words(0, "w_codes0")
        take_steps(1)

        u_codes = sb.tile([P, J], U32, align_bytes=64)
        u_plane = sb.tile([P, J], U8, align_bytes=64)
        u_half = []
        for h in range(2):
            u_half.append(sb.tile([P, HALF, PACK], BF16, name=f"u_half{h}", tag=f"u_half{h}", align_bytes=64))
            nc.vector.tensor_copy(
                out=u_half[h][:].rearrange("p j t -> p (j t)").bitcast(I32).rearrange("p (j i) -> p j i", i=2),
                in_=pairs[h][:].rearrange("p i j e -> p i (j e)").bitcast(I32).rearrange("p i j -> p j i"),
            )
        for h in range(2):
            cols = slice(h * HALF, (h + 1) * HALF)
            nc.vector.quantize_mx(
                out=u_codes[:, cols].bitcast(E4M3),
                scales=u_plane[:, cols],
                in_=u_half[h][:].rearrange("p j t -> p (j t)"),
            )

        deal_words(1, "u_half0")

        resid3 = sb.tile([P, N], F32)
        nc.scalar.activation(out=resid3[:], in_=resid[:], func=ACT.Copy, scale=0.3)

        a_rows = []
        for t in range(PACK):
            bank = ps.tile([P, J], F32, name=f"a_bank{t}")
            for cols in [slice(0, HALF), slice(HALF, J)] if t == 0 else [slice(0, J)]:
                nc.tensor.matmul_mx(
                    out=bank[:, cols],
                    lhsT=w_codes[t // 2][:, 2 * P * (t % 2) : 2 * P * (t % 2 + 1)].bitcast(E2M1),
                    lhsT_scale=w_plane[:, P * t : P * (t + 1)],
                    rhs=u_codes[:, cols].bitcast(E4M3),
                    rhs_scale=u_plane[:, cols],
                    start=True,
                    stop=True,
                )
            a_rows.append(sb.tile([P, J], F32, name=f"a_rows{t}", tag=f"a_rows{t}"))
            nc.scalar.activation(out=a_rows[t][:], in_=bank[:], func=ACT.Copy)

        look2 = sb.tile([P, PACK, O], F32)
        look3 = sb.tile([P, PACK, O], F32)
        for t in range(PACK):
            for e, (look, offsets) in enumerate(((look2, list2), (look3, list3))):
                window = a_rows[t][:].indirect(offsets[:])
                if 2 * t + e >= 5:
                    nc.scalar.activation(out=look[:, t, :], in_=window, func=ACT.Copy)
                else:
                    nc.vector.tensor_copy(out=look[:, t, :], in_=window)

        hid_codes = sb.tile([P, O], U32, align_bytes=64)
        hid_plane = sb.tile([P, O], U8, align_bytes=64)
        hid_half = []
        for h in range(2):
            cols = slice(h * (O // 2), (h + 1) * (O // 2))
            hid_half.append(sb.tile([P, O // 2, PACK], BF16, name=f"hid_half{h}", align_bytes=64))
            nc.vector.tensor_tensor(
                out=hid_half[h][:].rearrange("p (c i) t -> p c t i", i=4),
                in0=look2[:, :, cols].rearrange("p t (c i) -> p c t i", i=4),
                in1=look3[:, :, cols].rearrange("p t (c i) -> p c t i", i=4),
                op=ALU.max,
            )
        for h in range(2):
            cols = slice(h * (O // 2), (h + 1) * (O // 2))
            nc.vector.quantize_mx(
                out=hid_codes[:, cols].bitcast(E5M2),
                scales=hid_plane[:, cols],
                in_=hid_half[h][:].rearrange("p o t -> p (o t)"),
            )

        size = sb.tile([P, N], F32)
        prod = []
        for h in range(2):
            cols = slice(h * (N // 2), (h + 1) * (N // 2))
            prod.append(ps.tile([P, N // 2], F32, name=f"prod{h}"))
            nc.tensor.matmul_mx(
                out=prod[h][:],
                lhsT=hid_codes[:].bitcast(E5M2),
                lhsT_scale=hid_plane[:],
                rhs=wb_codes[:, cols].bitcast(E4M3),
                rhs_scale=wb_plane[:, cols],
                start=True,
                stop=True,
            )
            nc.scalar.activation(out=size[:, cols], in_=prod[h][:], func=ACT.Abs)
        lifted = sb.tile([P, N], F32)
        denom = sb.tile([P, 1], F32)
        nc.vector.tensor_scalar(
            out=lifted[:], in0=size[:], scalar1=0.2, scalar2=None, op0=ALU.add, op1=ALU.max,
            accum_out=denom[:],
        )
        inverse = sb.tile([P, 1], F32)
        nc.vector.reciprocal(out=inverse[:], in_=denom[:])
        for h, queue in enumerate((nc.scalar, nc.sync)):
            cols = slice(h * (N // 2), (h + 1) * (N // 2))
            result = sb.tile([P, N // 2], F32, name=f"result{h}")
            nc.vector.scalar_tensor_tensor(
                out=result[:], in0=prod[h][:], scalar=inverse[:], in1=resid3[:, cols],
                op0=ALU.mult, op1=ALU.add,
            )
            queue.dma_start(out=out[:, cols], in_=result[:])
